import numpy as np
import ml_dtypes


def mxq(x, axis, fmt="e4m3"):
    dtype, down = {"e4m3": (ml_dtypes.float8_e4m3fn, 7), "e5m2": (ml_dtypes.float8_e5m2, 14)}[fmt]
    v = np.moveaxis(np.asarray(x, np.float32).astype(ml_dtypes.bfloat16).astype(np.float64), axis, -1)
    blocks = v.reshape(v.shape[:-1] + (-1, 32))
    amax = np.abs(blocks).max(-1, keepdims=True)
    byte = np.maximum(np.where(amax > 0, np.frexp(amax)[1] - 1 + 127, 0) - down, 1)
    scale = np.exp2(byte - 127.0)
    codes = (blocks / scale).astype(np.float32).astype(dtype).astype(np.float64)
    return np.moveaxis((codes * scale).reshape(v.shape), -1, axis)


WIDE = False


def mx_kscale(k):
    if not WIDE:
        return np.ones(k)
    levels = np.array([10, -10, 5, -5, 0])
    if k % 512:
        return np.exp2(np.random.permutation(np.resize(levels, k // 32))).repeat(32)
    a = np.empty((k // 512, 16))
    for p in range(k // 512):
        a[p, :8] = np.random.permutation(np.resize(levels, 8))
        for g in range(8):
            far = levels[np.abs(levels - a[p, g]) >= 10]
            a[p, g + 8] = far[np.random.randint(len(far))]
    return np.exp2(a.ravel()).repeat(32)


def f64(x):
    return np.asarray(x).astype(np.float64)


def striped(idx):
    return np.tile(idx.reshape(-1, 16).T, (8, 1)).astype(np.uint16)


def unstriped(offs):
    return offs[:16].T.reshape(-1).astype(np.int64)


def striped8(idx):
    return np.concatenate([x.reshape(-1, 16).T for x in idx]).astype(np.uint16)


def runs(offs, k):
    lists = np.stack([offs[16 * r : 16 * r + 16].T.reshape(-1) for r in range(8)]).astype(np.int64)
    return lists[np.arange(k) % 512 // 64]


def pack_weight(w):
    k, n = w.shape
    w = f64(np.asarray(w, np.float32).astype(ml_dtypes.bfloat16)).reshape(k // 32, 32, n)
    amax = np.abs(w).max(1)
    byte = np.clip(np.where(amax > 0, np.frexp(amax)[1] - 1 + 127 - 7, 1), 1, 254)
    scaled = (w * np.exp2(127.0 - byte)[:, None, :]).reshape(k, n).astype(np.float32)
    words = np.ascontiguousarray(scaled.reshape(k // 512, 128, 4, n).transpose(0, 1, 3, 2)).astype(ml_dtypes.float8_e4m3fn).view(np.uint8)
    return words, np.ascontiguousarray(byte.astype(np.uint8).reshape(k // 512, 16, n))


def unpack_weight(words, scales):
    g, p, n, _ = words.shape
    vals = np.ascontiguousarray(words).view(ml_dtypes.float8_e4m3fn).astype(np.float64) * np.repeat(np.exp2(scales.astype(np.float64) - 127.0), 8, axis=1)[..., None]
    return vals.transpose(0, 1, 3, 2).reshape(g * 512, n)

def planes(y):
    n, m = y.shape
    v = y.astype(np.float32).astype(ml_dtypes.bfloat16).astype(np.float64).reshape(n // 32, 32, m)
    top = np.abs(v).max(1)
    byte = np.clip(np.where(top > 0, np.frexp(top)[1] - 1 + 127 - 7, 1), 1, 254)
    codes = (v * np.exp2(127.0 - byte)[:, None, :]).reshape(n, m).astype(np.float32).astype(ml_dtypes.float8_e4m3fn).view(np.uint8)
    words = codes.reshape(n // 512, 128, 4, m).transpose(0, 1, 3, 2)
    return np.ascontiguousarray(words), np.ascontiguousarray(byte.astype(np.uint8).reshape(n // 512, 16, m))


K, T, S, N, H, J, W = 512, 2048, 512, 512, 512, 512, 256


def setup_inputs():
    n = np.random.standard_normal
    s = mx_kscale(K)[:, None]
    u = mx_kscale(S)
    packed_xT = pack_weight(n((K, T)) * s)
    packed_w1 = pack_weight(n((S, N)) / np.sqrt(S) / u[:, None])
    perm = np.stack([np.random.permutation(H) for _ in range(8)])
    return {
        "x_words": packed_xT[0],
        "x_scales": packed_xT[1],
        "wa": (n((K, H)) / np.sqrt(K) / s).astype(np.float32),
        "tab": n((S, J)).astype(np.float32),
        "gt": (np.random.uniform(0.5, 1.5, (S, 1)) * u[:, None]).astype(np.float32),
        "w1_words": packed_w1[0],
        "w1_scales": packed_w1[1],
        "offs": striped(np.random.permutation(T)[:S]),
        "n1": striped8(np.random.randint(0, J, (8, H))),
        "n2": striped8(np.stack([np.random.permutation(H) for _ in range(8)])),
        "n3": striped8(perm[:, :W]),
        "n4": striped8(perm[:, W:]),
    }


def reference(x_words, x_scales, wa, tab, gt, w1_words, w1_scales, offs, n1, n2, n3, n4):
    xq = unpack_weight(x_words, x_scales)[:, unstriped(offs)]
    y = xq.T @ mxq(f64(wa), 0, "e4m3")
    z = f64(gt) * (np.abs(y - (y[np.arange(S)[:, None], runs(n2, S)]) - (f64(tab)[np.arange(S)[:, None], runs(n1, S)])))
    h = unpack_weight(w1_words, w1_scales).T @ mxq(z, 0, "e4m3")
    pa = h[np.arange(N)[:, None], runs(n3, N)]
    pb = h[np.arange(N)[:, None], runs(n4, N)]
    ra = np.maximum(pa, pb)
    out = h.copy()
    out[np.arange(N)[:, None], runs(n3, N)] = ra
    return (out,) + planes(out)

@@ -1,0 +1,285 @@
+from contextlib import ExitStack
+
+import concourse.mybir as mybir
+
+F32 = mybir.dt.float32
+BF16 = mybir.dt.bfloat16
+I32 = mybir.dt.int32
+U32 = mybir.dt.uint32
+U16 = mybir.dt.uint16
+U8 = mybir.dt.uint8
+FP8X4 = mybir.dt.float8_e4m3fn_x4
+ALU = mybir.AluOpType
+ACT = mybir.ActivationFunctionType
+
+P = 128
+PACK = 4
+T = 2048
+D = 512
+W = 256
+HALF = D // 2
+LIST = 16
+FLOPS = 2 * 2 * D * D * D
+Z_CHUNKS = ((0, 256), (256, 128), (384, 128))
+H_ORDER = (2, 0, 1, 3)
+LAST_SPLIT = 352
+
+
+def tile_picked_tokkinddfill_none_po_kernel(
+    tc, x_words, x_scales, wa, tab, gt, w1_words, w1_scales, offs, n1, n2, n3, n4, out_0, out_1, out_2
+):
+    nc = tc.nc
+    with ExitStack() as ctx:
+        lists = ctx.enter_context(tc.tile_pool(name="lists", bufs=1))
+        keep = ctx.enter_context(tc.tile_pool(name="keep", bufs=1))
+        ring = ctx.enter_context(tc.tile_pool(name="ring", bufs=3))
+        psum = ctx.enter_context(tc.psum_pool(name="psum", bufs=1))
+
+        def tile(name, shape, dtype, tag=""):
+            return keep.tile(shape, dtype, name=name, tag=tag or name, align_bytes=64)
+
+        def cols(lst, start, width):
+            return lst[:, start // LIST : (start + width) // LIST]
+
+        def load_scale_rows(queue, plane, rows):
+            for q in range(4):
+                queue.dma_start(out=plane[32 * q : 32 * q + 4, :].bitcast(I32), in_=rows[0, 4 * q : 4 * q + 4, :].bitcast(I32))
+
+        def words_view(words):
+            return words[0].rearrange("p c r -> p (c r)").bitcast(I32)
+
+        def deal(dst, src):
+            nc.vector.tensor_copy(
+                out=dst[:].rearrange("p (t c i) -> p c t i", t=PACK, i=4),
+                in_=src[:].rearrange("p (c i t) -> p c t i", t=PACK, i=4),
+            )
+
+        def weave_views(dst, src):
+            return (
+                dst.rearrange("p (c i t) -> p c t i", t=PACK, i=4),
+                src.rearrange("p t (c i) -> p c t i", i=4),
+            )
+
+        offs_sb = lists.tile([P, D // LIST], U16, name="offs_sb")
+        n1_sb = lists.tile([P, D // LIST], U16, name="n1_sb")
+        n2_sb = lists.tile([P, D // LIST], U16, name="n2_sb")
+        n3_sb = lists.tile([P, W // LIST], U16, name="n3_sb")
+        n4_sb = lists.tile([P, W // LIST], U16, name="n4_sb")
+
+        xs_all = tile("xs_all", [P, T], U8)
+        w1s_raw = tile("w1s_raw", [P, D], U8)
+        nc.gpsimd.memset(xs_all[:].bitcast(I32), 0)
+        nc.vector.memset(w1s_raw[:].bitcast(I32), 0)
+
+        tab_rows = tab.rearrange("(p t) j -> p t j", t=PACK)
+        wa_rows = wa.rearrange("(p t) j -> p t j", t=PACK)
+        tab_sb = [tile(f"tab{t}", [P, D], F32) for t in range(PACK)]
+        wa_sb = [tile(f"wa{u}", [P, PACK, HALF], F32) for u in range(2)]
+        xw_all = tile("xw_all", [P, T], I32)
+        w1w_raw = tile("w1w_raw", [P, D], I32)
+        gt_sb = tile("gt_sb", [P, PACK], F32)
+
+        load_scale_rows(nc.gpsimd, xs_all, x_scales)
+        nc.sync.dma_start(out=n1_sb[:], in_=n1)
+        nc.sync.dma_start(out=tab_sb[0][:], in_=tab_rows[:, 0, :])
+        nc.sync.dma_start(out=tab_sb[1][:], in_=tab_rows[:, 1, :])
+        nc.sync.dma_start(out=wa_sb[0][:], in_=wa_rows[:, :, :HALF])
+        nc.sync.dma_start(out=tab_sb[2][:], in_=tab_rows[:, 2, :])
+        nc.sync.dma_start(out=wa_sb[1][:], in_=wa_rows[:, :, HALF:])
+        nc.sync.dma_start(out=offs_sb[:], in_=offs)
+        nc.sync.dma_start(out=xw_all[:], in_=words_view(x_words))
+        nc.sync.dma_start(out=gt_sb[:], in_=gt.rearrange("(p t) o -> p (t o)", t=PACK))
+        nc.sync.dma_start(out=tab_sb[3][:], in_=tab_rows[:, 3, :])
+        nc.sync.dma_start(out=w1w_raw[:], in_=words_view(w1_words))
+        nc.sync.dma_start(out=n2_sb[:], in_=n2)
+        load_scale_rows(nc.sync, w1s_raw, w1_scales)
+        nc.sync.dma_start(out=n3_sb[:], in_=n3)
+        nc.sync.dma_start(out=n4_sb[:], in_=n4)
+
+        sign = tile("sign", [P, HALF, PACK], BF16)
+        nc.scalar.activation(out=sign[:], in_=gt_sb[:].unsqueeze(1).to_broadcast([P, HALF, PACK]), func=ACT.Sign)
+
+        kinds = {}
+
+        def gather_kinds(t):
+            for u in range(2):
+                nc.vector.tensor_copy(
+                    out=kinds[t][:, u * HALF : (u + 1) * HALF],
+                    in_=tab_sb[t][:].indirect(cols(n1_sb, u * HALF, HALF)),
+                )
+
+        xs_dealt = tile("xs_dealt", [P, D], U8)
+        xw_dealt = tile("xw_dealt", [P, D], U32)
+        wa_bf = [tile(f"wa_bf{u}", [P, HALF * PACK], BF16) for u in range(2)]
+        wa_codes = tile("wa_codes", [P, D], U32)
+        wa_scales = tile("wa_scales", [P, D], U8)
+        w1s = tile("w1s", [P, D], U8)
+        w1w = tile("w1w", [P, D], I32)
+
+        def quantize_wa(u):
+            dst, src = weave_views(wa_bf[u][:], wa_sb[u][:])
+            nc.scalar.copy(out=dst, in_=src)
+            half = slice(u * HALF, (u + 1) * HALF)
+            nc.vector.quantize_mx(out=wa_codes[:, half].bitcast(FP8X4), scales=wa_scales[:, half], in_=wa_bf[u][:])
+
+        for t in range(PACK - 1):
+            kinds[t] = tile(f"kinds{t}", [P, D], F32)
+            gather_kinds(t)
+        quantize_wa(0)
+        xs_picked = tile("xs_picked", [P, D], U8, tag="picked")
+        nc.vector.tensor_copy(out=xs_picked[:], in_=xs_all[:].indirect(offs_sb[:]))
+        quantize_wa(1)
+        deal(xs_dealt, xs_picked)
+        xw_picked = tile("xw_picked", [P, D], U32, tag="picked")
+        nc.vector.tensor_copy(out=xw_picked[:], in_=xw_all[:].bitcast(U32).indirect(offs_sb[:]))
+        deal(xw_dealt, xw_picked)
+        kinds[PACK - 1] = tile("kinds_last", [P, D], F32, tag="picked")
+        gather_kinds(PACK - 1)
+        deal(w1w, w1w_raw)
+        deal(w1s, w1s_raw)
+
+        gy = [tile(f"gy{t}", [P, D], F32) for t in range(PACK)]
+        rest = [tile(f"rest{t}", [P, D], F32) for t in range(PACK)]
+        for t in range(PACK):
+            rows = slice(t * P, (t + 1) * P)
+            y_ps = psum.tile([P, D], F32, name=f"y_ps{t}")
+            nc.tensor.matmul_mx(
+                out=y_ps[:],
+                lhsT=xw_dealt[:, rows].bitcast(FP8X4),
+                lhsT_scale=xs_dealt[:, rows],
+                rhs=wa_codes[:].bitcast(FP8X4),
+                rhs_scale=wa_scales[:],
+                start=True,
+                stop=True,
+            )
+            nc.scalar.activation(out=gy[t][:], in_=y_ps[:], func=ACT.Copy, scale=gt_sb[:, t : t + 1])
+
+        def make_rest(t):
+            nc.vector.scalar_tensor_tensor(
+                out=rest[t][:], in0=kinds[t][:], scalar=gt_sb[:, t : t + 1], in1=gy[t][:], op0=ALU.mult, op1=ALU.subtract
+            )
+
+        diff = [tile(f"diff{c}", [P, PACK, w], F32) for c, (s, w) in enumerate(Z_CHUNKS)]
+        size = [tile(f"size{c}", [P, w * PACK], BF16) for c, (s, w) in enumerate(Z_CHUNKS)]
+        z_bf = [tile(f"z_bf{c}", [P, w * PACK], BF16) for c, (s, w) in enumerate(Z_CHUNKS)]
+        z_codes = [tile(f"z_codes{c}", [P, w], U32) for c, (s, w) in enumerate(Z_CHUNKS)]
+        z_scales = [tile(f"z_scales{c}", [P, w], U8) for c, (s, w) in enumerate(Z_CHUNKS)]
+        h_ps = [psum.tile([P, D], F32, name=f"h_ps{t}") for t in range(PACK)]
+        h_sb = [tile(f"h_sb{t}", [P, D], F32) for t in range(PACK)]
+
+        def gather_diff(c, t):
+            s, w = Z_CHUNKS[c]
+            nc.vector.tensor_tensor(
+                out=diff[c][:, t, :], in0=gy[t][:].indirect(cols(n2_sb, s, w)), in1=rest[t][:, s : s + w], op=ALU.add
+            )
+
+        def take_size(c):
+            dst, src = weave_views(size[c][:], diff[c][:])
+            nc.scalar.activation(out=dst, in_=src, func=ACT.Abs)
+
+        def apply_sign(c):
+            s, w = Z_CHUNKS[c]
+            nc.vector.tensor_tensor(
+                out=z_bf[c][:], in0=size[c][:], in1=sign[:, :w, :].rearrange("p j t -> p (j t)"), op=ALU.mult
+            )
+
+        def second_product(c):
+            s, w = Z_CHUNKS[c]
+            nc.vector.quantize_mx(out=z_codes[c][:].bitcast(FP8X4), scales=z_scales[c][:], in_=z_bf[c][:])
+            for t in H_ORDER:
+                rows = slice(t * P, (t + 1) * P)
+                nc.tensor.matmul_mx(
+                    out=h_ps[t][:, s : s + w],
+                    lhsT=w1w[:, rows].bitcast(FP8X4),
+                    lhsT_scale=w1s[:, rows],
+                    rhs=z_codes[c][:].bitcast(FP8X4),
+                    rhs_scale=z_scales[c][:],
+                    start=True,
+                    stop=True,
+                )
+
+        make_rest(0)
+        for t in range(PACK):
+            if t + 1 < PACK:
+                make_rest(t + 1)
+            gather_diff(0, t)
+        take_size(0)
+        for t in range(PACK):
+            gather_diff(1, t)
+        take_size(1)
+        apply_sign(0)
+        gather_diff(2, 0)
+        second_product(0)
+        for t in range(1, PACK):
+            gather_diff(2, t)
+        for t in H_ORDER:
+            nc.scalar.copy(out=h_sb[t][:, :HALF], in_=h_ps[t][:, :HALF])
+        take_size(2)
+        apply_sign(1)
+        second_product(1)
+        apply_sign(2)
+        second_product(2)
+
+        pa = [tile(f"pa{t}", [P, W], F32) for t in range(PACK)]
+        pb = [tile(f"pb{t}", [P, W], F32) for t in range(PACK)]
+        ra = [tile(f"ra{t}", [P, W], F32) for t in range(PACK)]
+        out_bf = tile("out_bf", [P, D, PACK], BF16)
+        out_rows = out_0.rearrange("(p t) j -> p t j", t=PACK)
+        placed = {}
+
+        def leave_psum(t):
+            nc.scalar.copy(out=h_sb[t][:, HALF:], in_=h_ps[t][:, HALF:])
+
+        def fill_window(t):
+            placed[t] = ring.tile([P, D], F32, name="placed")
+            nc.scalar.copy(out=placed[t][:], in_=h_ps[t][:])
+
+        def gather_a(t):
+            nc.vector.tensor_copy(out=pa[t][:], in_=h_sb[t][:].indirect(n3_sb[:]))
+
+        def gather_b(t):
+            nc.vector.tensor_copy(out=pb[t][:], in_=h_sb[t][:].indirect(n4_sb[:]))
+
+        def larger(t):
+            nc.vector.tensor_tensor(out=ra[t][:], in0=pa[t][:], in1=pb[t][:], op=ALU.max)
+
+        def place(t):
+            nc.vector.tensor_copy(out=placed[t][:].indirect(n3_sb[:]), in_=ra[t][:])
+            nc.sync.dma_start(out=out_rows[:, t, :], in_=placed[t][:])
+
+        for t in H_ORDER:
+            leave_psum(t)
+        gather_a(H_ORDER[0])
+        gather_b(H_ORDER[0])
+        for n, t in enumerate(H_ORDER):
+            after = H_ORDER[n + 1] if n + 1 < PACK else None
+            fill_window(t)
+            if after is not None:
+                gather_a(after)
+            larger(t)
+            if after is not None:
+                gather_b(after)
+            place(t)
+            if after is not None:
+                nc.scalar.copy(out=out_bf[:, :, t], in_=placed[t][:])
+
+        last = H_ORDER[-1]
+        nc.vector.tensor_copy(out=out_bf[:, :HALF, last], in_=placed[last][:, :HALF])
+        nc.vector.tensor_copy(out=out_bf[:, HALF:LAST_SPLIT, last], in_=placed[last][:, HALF:LAST_SPLIT])
+        nc.scalar.copy(out=out_bf[:, LAST_SPLIT:, last], in_=placed[last][:, LAST_SPLIT:])
+
+        out_codes = tile("out_codes", [P, D], I32)
+        out_scales = tile("out_scales", [P, D], U8)
+        for u, queue in enumerate((nc.sync, nc.scalar)):
+            half = slice(u * HALF, (u + 1) * HALF)
+            nc.vector.quantize_mx(
+                out=out_codes[:, half].bitcast(FP8X4),
+                scales=out_scales[:, half],
+                in_=out_bf[:, half, :].rearrange("p j t -> p (j t)"),
+            )
+            queue.dma_start(out=words_view(out_1)[:, half], in_=out_codes[:, half])
+        for q in range(4):
+            queue = (nc.sync, nc.scalar)[q % 2]
+            queue.dma_start(
+                out=out_2[0, 4 * q : 4 * q + 4, :].bitcast(I32), in_=out_scales[32 * q : 32 * q + 4, :].bitcast(I32)
+            )

@@ -32,7 +32,6 @@ def tile_picked_tokkinddfill_none_po_kernel(
     with ExitStack() as ctx:
         lists = ctx.enter_context(tc.tile_pool(name="lists", bufs=1))
         keep = ctx.enter_context(tc.tile_pool(name="keep", bufs=1))
-        ring = ctx.enter_context(tc.tile_pool(name="ring", bufs=3))
         psum = ctx.enter_context(tc.psum_pool(name="psum", bufs=1))
 
         def tile(name, shape, dtype, tag=""):
@@ -69,7 +68,7 @@ def tile_picked_tokkinddfill_none_po_kernel(
         xs_all = tile("xs_all", [P, T], U8)
         w1s_raw = tile("w1s_raw", [P, D], U8)
         nc.gpsimd.memset(xs_all[:].bitcast(I32), 0)
-        nc.vector.memset(w1s_raw[:].bitcast(I32), 0)
+        nc.gpsimd.memset(w1s_raw[:].bitcast(I32), 0)
 
         tab_rows = tab.rearrange("(p t) j -> p t j", t=PACK)
         wa_rows = wa.rearrange("(p t) j -> p t j", t=PACK)
@@ -79,14 +78,14 @@ def tile_picked_tokkinddfill_none_po_kernel(
         w1w_raw = tile("w1w_raw", [P, D], I32)
         gt_sb = tile("gt_sb", [P, PACK], F32)
 
-        load_scale_rows(nc.gpsimd, xs_all, x_scales)
         nc.sync.dma_start(out=n1_sb[:], in_=n1)
         nc.sync.dma_start(out=tab_sb[0][:], in_=tab_rows[:, 0, :])
+        load_scale_rows(nc.sync, xs_all, x_scales)
         nc.sync.dma_start(out=tab_sb[1][:], in_=tab_rows[:, 1, :])
         nc.sync.dma_start(out=wa_sb[0][:], in_=wa_rows[:, :, :HALF])
+        nc.sync.dma_start(out=offs_sb[:], in_=offs)
         nc.sync.dma_start(out=tab_sb[2][:], in_=tab_rows[:, 2, :])
         nc.sync.dma_start(out=wa_sb[1][:], in_=wa_rows[:, :, HALF:])
-        nc.sync.dma_start(out=offs_sb[:], in_=offs)
         nc.sync.dma_start(out=xw_all[:], in_=words_view(x_words))
         nc.sync.dma_start(out=gt_sb[:], in_=gt.rearrange("(p t) o -> p (t o)", t=PACK))
         nc.sync.dma_start(out=tab_sb[3][:], in_=tab_rows[:, 3, :])
@@ -124,12 +123,14 @@ def tile_picked_tokkinddfill_none_po_kernel(
 
         for t in range(PACK - 1):
             kinds[t] = tile(f"kinds{t}", [P, D], F32)
-            gather_kinds(t)
-        quantize_wa(0)
+        gather_kinds(0)
+        gather_kinds(1)
         xs_picked = tile("xs_picked", [P, D], U8, tag="picked")
         nc.vector.tensor_copy(out=xs_picked[:], in_=xs_all[:].indirect(offs_sb[:]))
-        quantize_wa(1)
+        gather_kinds(2)
         deal(xs_dealt, xs_picked)
+        quantize_wa(0)
+        quantize_wa(1)
         xw_picked = tile("xw_picked", [P, D], U32, tag="picked")
         nc.vector.tensor_copy(out=xw_picked[:], in_=xw_all[:].bitcast(U32).indirect(offs_sb[:]))
         deal(xw_dealt, xw_picked)
@@ -212,8 +213,8 @@ def tile_picked_tokkinddfill_none_po_kernel(
         second_product(0)
         for t in range(1, PACK):
             gather_diff(2, t)
-        for t in H_ORDER:
-            nc.scalar.copy(out=h_sb[t][:, :HALF], in_=h_ps[t][:, :HALF])
+        first, last = H_ORDER[0], H_ORDER[-1]
+        nc.scalar.copy(out=h_sb[first][:, :HALF], in_=h_ps[first][:, :HALF])
         take_size(2)
         apply_sign(1)
         second_product(1)
@@ -228,10 +229,10 @@ def tile_picked_tokkinddfill_none_po_kernel(
         placed = {}
 
         def leave_psum(t):
-            nc.scalar.copy(out=h_sb[t][:, HALF:], in_=h_ps[t][:, HALF:])
+            nc.scalar.copy(out=h_sb[t][:], in_=h_ps[t][:])
 
         def fill_window(t):
-            placed[t] = ring.tile([P, D], F32, name="placed")
+            placed[t] = tile(f"placed{t}", [P, D], F32, tag=f"ra{H_ORDER[0]}" if t == H_ORDER[-1] else "")
             nc.scalar.copy(out=placed[t][:], in_=h_ps[t][:])
 
         def gather_a(t):
@@ -247,23 +248,24 @@ def tile_picked_tokkinddfill_none_po_kernel(
             nc.vector.tensor_copy(out=placed[t][:].indirect(n3_sb[:]), in_=ra[t][:])
             nc.sync.dma_start(out=out_rows[:, t, :], in_=placed[t][:])
 
-        for t in H_ORDER:
+        nc.scalar.copy(out=h_sb[first][:, HALF:], in_=h_ps[first][:, HALF:])
+        for t in H_ORDER[1:]:
             leave_psum(t)
-        gather_a(H_ORDER[0])
-        gather_b(H_ORDER[0])
-        for n, t in enumerate(H_ORDER):
-            after = H_ORDER[n + 1] if n + 1 < PACK else None
+        gather_a(first)
+        gather_b(first)
+        for t in H_ORDER[:-1]:
             fill_window(t)
-            if after is not None:
-                gather_a(after)
+        for t, after in zip(H_ORDER, H_ORDER[1:]):
+            gather_a(after)
             larger(t)
-            if after is not None:
-                gather_b(after)
+            gather_b(after)
             place(t)
-            if after is not None:
-                nc.scalar.copy(out=out_bf[:, :, t], in_=placed[t][:])
+            nc.scalar.copy(out=out_bf[:, :, t], in_=placed[t][:])
+            if t == first:
+                fill_window(last)
+        larger(last)
+        place(last)
 
-        last = H_ORDER[-1]
         nc.vector.tensor_copy(out=out_bf[:, :HALF, last], in_=placed[last][:, :HALF])
         nc.vector.tensor_copy(out=out_bf[:, HALF:LAST_SPLIT, last], in_=placed[last][:, HALF:LAST_SPLIT])
         nc.scalar.copy(out=out_bf[:, LAST_SPLIT:, last], in_=placed[last][:, LAST_SPLIT:])

@@ -23,6 +23,7 @@ FLOPS = 2 * 2 * D * D * D
 Z_CHUNKS = ((0, 256), (256, 128), (384, 128))
 H_ORDER = (2, 0, 1, 3)
 LAST_SPLIT = 352
+EARLY = 3
 
 
 def tile_picked_tokkinddfill_none_po_kernel(
@@ -41,8 +42,8 @@ def tile_picked_tokkinddfill_none_po_kernel(
             return lst[:, start // LIST : (start + width) // LIST]
 
         def load_scale_rows(queue, plane, rows):
-            for q in range(4):
-                queue.dma_start(out=plane[32 * q : 32 * q + 4, :].bitcast(I32), in_=rows[0, 4 * q : 4 * q + 4, :].bitcast(I32))
+            for r in range(4):
+                queue.dma_start(out=plane[r:P:32, :].bitcast(I32), in_=rows[0, r:16:4, :].bitcast(I32))
 
         def words_view(words):
             return words[0].rearrange("p c r -> p (c r)").bitcast(I32)
@@ -73,7 +74,7 @@ def tile_picked_tokkinddfill_none_po_kernel(
         tab_rows = tab.rearrange("(p t) j -> p t j", t=PACK)
         wa_rows = wa.rearrange("(p t) j -> p t j", t=PACK)
         tab_sb = [tile(f"tab{t}", [P, D], F32) for t in range(PACK)]
-        wa_sb = [tile(f"wa{u}", [P, PACK, HALF], F32) for u in range(2)]
+        wa_sb = tile("wa_sb", [P, PACK, D], F32)
         xw_all = tile("xw_all", [P, T], I32)
         w1w_raw = tile("w1w_raw", [P, D], I32)
         gt_sb = tile("gt_sb", [P, PACK], F32)
@@ -82,21 +83,17 @@ def tile_picked_tokkinddfill_none_po_kernel(
         nc.sync.dma_start(out=tab_sb[0][:], in_=tab_rows[:, 0, :])
         load_scale_rows(nc.sync, xs_all, x_scales)
         nc.sync.dma_start(out=tab_sb[1][:], in_=tab_rows[:, 1, :])
-        nc.sync.dma_start(out=wa_sb[0][:], in_=wa_rows[:, :, :HALF])
+        nc.sync.dma_start(out=wa_sb[:], in_=wa_rows)
         nc.sync.dma_start(out=offs_sb[:], in_=offs)
-        nc.sync.dma_start(out=tab_sb[2][:], in_=tab_rows[:, 2, :])
-        nc.sync.dma_start(out=wa_sb[1][:], in_=wa_rows[:, :, HALF:])
         nc.sync.dma_start(out=xw_all[:], in_=words_view(x_words))
+        nc.sync.dma_start(out=tab_sb[2][:], in_=tab_rows[:, 2, :])
         nc.sync.dma_start(out=gt_sb[:], in_=gt.rearrange("(p t) o -> p (t o)", t=PACK))
         nc.sync.dma_start(out=tab_sb[3][:], in_=tab_rows[:, 3, :])
         nc.sync.dma_start(out=w1w_raw[:], in_=words_view(w1_words))
-        nc.sync.dma_start(out=n2_sb[:], in_=n2)
         load_scale_rows(nc.sync, w1s_raw, w1_scales)
+        nc.sync.dma_start(out=n2_sb[:], in_=n2)
         nc.sync.dma_start(out=n3_sb[:], in_=n3)
         nc.sync.dma_start(out=n4_sb[:], in_=n4)
-
-        sign = tile("sign", [P, HALF, PACK], BF16)
-        nc.scalar.activation(out=sign[:], in_=gt_sb[:].unsqueeze(1).to_broadcast([P, HALF, PACK]), func=ACT.Sign)
 
         kinds = {}
 
@@ -116,26 +113,25 @@ def tile_picked_tokkinddfill_none_po_kernel(
         w1w = tile("w1w", [P, D], I32)
 
         def quantize_wa(u):
-            dst, src = weave_views(wa_bf[u][:], wa_sb[u][:])
-            nc.scalar.copy(out=dst, in_=src)
             half = slice(u * HALF, (u + 1) * HALF)
+            dst, src = weave_views(wa_bf[u][:], wa_sb[:, :, half])
+            nc.scalar.copy(out=dst, in_=src)
             nc.vector.quantize_mx(out=wa_codes[:, half].bitcast(FP8X4), scales=wa_scales[:, half], in_=wa_bf[u][:])
 
-        for t in range(PACK - 1):
+        for t in range(EARLY - 1):
             kinds[t] = tile(f"kinds{t}", [P, D], F32)
         gather_kinds(0)
         gather_kinds(1)
         xs_picked = tile("xs_picked", [P, D], U8, tag="picked")
         nc.vector.tensor_copy(out=xs_picked[:], in_=xs_all[:].indirect(offs_sb[:]))
-        gather_kinds(2)
-        deal(xs_dealt, xs_picked)
         quantize_wa(0)
-        quantize_wa(1)
+        deal(xs_dealt, xs_picked)
         xw_picked = tile("xw_picked", [P, D], U32, tag="picked")
         nc.vector.tensor_copy(out=xw_picked[:], in_=xw_all[:].bitcast(U32).indirect(offs_sb[:]))
+        quantize_wa(1)
         deal(xw_dealt, xw_picked)
-        kinds[PACK - 1] = tile("kinds_last", [P, D], F32, tag="picked")
-        gather_kinds(PACK - 1)
+        kinds[EARLY - 1] = tile("kinds_last", [P, D], F32, tag="picked")
+        gather_kinds(EARLY - 1)
         deal(w1w, w1w_raw)
         deal(w1s, w1s_raw)
 
@@ -143,7 +139,7 @@ def tile_picked_tokkinddfill_none_po_kernel(
         rest = [tile(f"rest{t}", [P, D], F32) for t in range(PACK)]
         for t in range(PACK):
             rows = slice(t * P, (t + 1) * P)
-            y_ps = psum.tile([P, D], F32, name=f"y_ps{t}")
+            y_ps = psum.tile([P, D], F32, name=f"y_ps{t}", tag=f"y_ps{t}")
             nc.tensor.matmul_mx(
                 out=y_ps[:],
                 lhsT=xw_dealt[:, rows].bitcast(FP8X4),
@@ -155,17 +151,37 @@ def tile_picked_tokkinddfill_none_po_kernel(
             )
             nc.scalar.activation(out=gy[t][:], in_=y_ps[:], func=ACT.Copy, scale=gt_sb[:, t : t + 1])
 
+        gtab = {}
+        for t in range(EARLY, PACK):
+            gtab[t] = tile(f"gtab{t}", [P, D], F32)
+            nc.scalar.activation(out=gtab[t][:], in_=tab_sb[t][:], func=ACT.Copy, scale=gt_sb[:, t : t + 1])
+
+        sign = tile("sign", [P, HALF, PACK], BF16)
+        nc.scalar.activation(out=sign[:], in_=gt_sb[:].unsqueeze(1).to_broadcast([P, HALF, PACK]), func=ACT.Sign)
+
         def make_rest(t):
-            nc.vector.scalar_tensor_tensor(
-                out=rest[t][:], in0=kinds[t][:], scalar=gt_sb[:, t : t + 1], in1=gy[t][:], op0=ALU.mult, op1=ALU.subtract
-            )
+            if t < EARLY:
+                nc.vector.scalar_tensor_tensor(
+                    out=rest[t][:], in0=kinds[t][:], scalar=gt_sb[:, t : t + 1], in1=gy[t][:], op0=ALU.mult, op1=ALU.subtract
+                )
+            else:
+                for u in range(2):
+                    half = slice(u * HALF, (u + 1) * HALF)
+                    nc.vector.tensor_tensor(
+                        out=rest[t][:, half],
+                        in0=gtab[t][:].indirect(cols(n1_sb, u * HALF, HALF)),
+                        in1=gy[t][:, half],
+                        op=ALU.subtract,
+                    )
 
         diff = [tile(f"diff{c}", [P, PACK, w], F32) for c, (s, w) in enumerate(Z_CHUNKS)]
         size = [tile(f"size{c}", [P, w * PACK], BF16) for c, (s, w) in enumerate(Z_CHUNKS)]
         z_bf = [tile(f"z_bf{c}", [P, w * PACK], BF16) for c, (s, w) in enumerate(Z_CHUNKS)]
         z_codes = [tile(f"z_codes{c}", [P, w], U32) for c, (s, w) in enumerate(Z_CHUNKS)]
         z_scales = [tile(f"z_scales{c}", [P, w], U8) for c, (s, w) in enumerate(Z_CHUNKS)]
-        h_ps = [psum.tile([P, D], F32, name=f"h_ps{t}") for t in range(PACK)]
+        first, last = H_ORDER[0], H_ORDER[-1]
+        h_ps = {t: psum.tile([P, D], F32, name=f"h_ps{t}") for t in H_ORDER[1:]}
+        h_first = [psum.tile([P, w], F32, name=f"h_first{c}", tag=f"y_ps{c}") for c, (s, w) in enumerate(Z_CHUNKS)]
         h_sb = [tile(f"h_sb{t}", [P, D], F32) for t in range(PACK)]
 
         def gather_diff(c, t):
@@ -190,7 +206,7 @@ def tile_picked_tokkinddfill_none_po_kernel(
             for t in H_ORDER:
                 rows = slice(t * P, (t + 1) * P)
                 nc.tensor.matmul_mx(
-                    out=h_ps[t][:, s : s + w],
+                    out=h_first[c][:] if t == first else h_ps[t][:, s : s + w],
                     lhsT=w1w[:, rows].bitcast(FP8X4),
                     lhsT_scale=w1s[:, rows],
                     rhs=z_codes[c][:].bitcast(FP8X4),
@@ -198,6 +214,10 @@ def tile_picked_tokkinddfill_none_po_kernel(
                     start=True,
                     stop=True,
                 )
+
+        def leave_early(c):
+            s, w = Z_CHUNKS[c]
+            nc.scalar.copy(out=h_sb[first][:, s : s + w], in_=h_first[c][:])
 
         make_rest(0)
         for t in range(PACK):
@@ -213,13 +233,14 @@ def tile_picked_tokkinddfill_none_po_kernel(
         second_product(0)
         for t in range(1, PACK):
             gather_diff(2, t)
-        first, last = H_ORDER[0], H_ORDER[-1]
-        nc.scalar.copy(out=h_sb[first][:, :HALF], in_=h_ps[first][:, :HALF])
+        leave_early(0)
         take_size(2)
         apply_sign(1)
         second_product(1)
+        leave_early(1)
         apply_sign(2)
         second_product(2)
+        leave_early(2)
 
         pa = [tile(f"pa{t}", [P, W], F32) for t in range(PACK)]
         pb = [tile(f"pb{t}", [P, W], F32) for t in range(PACK)]
@@ -233,7 +254,7 @@ def tile_picked_tokkinddfill_none_po_kernel(
 
         def fill_window(t):
             placed[t] = tile(f"placed{t}", [P, D], F32, tag=f"ra{H_ORDER[0]}" if t == H_ORDER[-1] else "")
-            nc.scalar.copy(out=placed[t][:], in_=h_ps[t][:])
+            nc.scalar.copy(out=placed[t][:], in_=h_sb[t][:])
 
         def gather_a(t):
             nc.vector.tensor_copy(out=pa[t][:], in_=h_sb[t][:].indirect(n3_sb[:]))
@@ -248,22 +269,34 @@ def tile_picked_tokkinddfill_none_po_kernel(
             nc.vector.tensor_copy(out=placed[t][:].indirect(n3_sb[:]), in_=ra[t][:])
             nc.sync.dma_start(out=out_rows[:, t, :], in_=placed[t][:])
 
-        nc.scalar.copy(out=h_sb[first][:, HALF:], in_=h_ps[first][:, HALF:])
         for t in H_ORDER[1:]:
             leave_psum(t)
         gather_a(first)
         gather_b(first)
         for t in H_ORDER[:-1]:
             fill_window(t)
-        for t, after in zip(H_ORDER, H_ORDER[1:]):
-            gather_a(after)
-            larger(t)
-            gather_b(after)
-            place(t)
+        second, third = H_ORDER[1], H_ORDER[2]
+
+        def regroup(t):
             nc.scalar.copy(out=out_bf[:, :, t], in_=placed[t][:])
-            if t == first:
-                fill_window(last)
+
+        gather_a(second)
+        larger(first)
+        gather_b(second)
+        place(first)
+        regroup(first)
+        fill_window(last)
+        gather_a(third)
+        larger(second)
+        gather_b(third)
+        gather_a(last)
+        larger(third)
+        gather_b(last)
+        place(second)
+        regroup(second)
         larger(last)
+        place(third)
+        regroup(third)
         place(last)
 
         nc.vector.tensor_copy(out=out_bf[:, :HALF, last], in_=placed[last][:, :HALF])

from contextlib import ExitStack

import concourse.mybir as mybir

F32 = mybir.dt.float32
BF16 = mybir.dt.bfloat16
I32 = mybir.dt.int32
U32 = mybir.dt.uint32
U16 = mybir.dt.uint16
U8 = mybir.dt.uint8
FP8X4 = mybir.dt.float8_e4m3fn_x4
ALU = mybir.AluOpType
ACT = mybir.ActivationFunctionType

P = 128
PACK = 4
T = 2048
D = 512
W = 256
HALF = D // 2
LIST = 16
FLOPS = 2 * 2 * D * D * D
Z_CHUNKS = ((0, 256), (256, 128), (384, 128))
H_ORDER = (2, 0, 1, 3)
LAST_SPLIT = 352
EARLY = 3


def tile_picked_tokkinddfill_none_po_kernel(
    tc, x_words, x_scales, wa, tab, gt, w1_words, w1_scales, offs, n1, n2, n3, n4, out_0, out_1, out_2
):
    nc = tc.nc
    with ExitStack() as ctx:
        lists = ctx.enter_context(tc.tile_pool(name="lists", bufs=1))
        keep = ctx.enter_context(tc.tile_pool(name="keep", bufs=1))
        psum = ctx.enter_context(tc.psum_pool(name="psum", bufs=1))

        def tile(name, shape, dtype, tag=""):
            return keep.tile(shape, dtype, name=name, tag=tag or name, align_bytes=64)

        def cols(lst, start, width):
            return lst[:, start // LIST : (start + width) // LIST]

        def load_scale_rows(queue, plane, rows):
            for r in range(4):
                queue.dma_start(out=plane[r:P:32, :].bitcast(I32), in_=rows[0, r:16:4, :].bitcast(I32))

        def words_view(words):
            return words[0].rearrange("p c r -> p (c r)").bitcast(I32)

        def deal(dst, src):
            nc.vector.tensor_copy(
                out=dst[:].rearrange("p (t c i) -> p c t i", t=PACK, i=4),
                in_=src[:].rearrange("p (c i t) -> p c t i", t=PACK, i=4),
            )

        def weave_views(dst, src):
            return (
                dst.rearrange("p (c i t) -> p c t i", t=PACK, i=4),
                src.rearrange("p t (c i) -> p c t i", i=4),
            )

        offs_sb = lists.tile([P, D // LIST], U16, name="offs_sb")
        n1_sb = lists.tile([P, D // LIST], U16, name="n1_sb")
        n2_sb = lists.tile([P, D // LIST], U16, name="n2_sb")
        n3_sb = lists.tile([P, W // LIST], U16, name="n3_sb")
        n4_sb = lists.tile([P, W // LIST], U16, name="n4_sb")

        xs_all = tile("xs_all", [P, T], U8)
        w1s_raw = tile("w1s_raw", [P, D], U8)
        nc.gpsimd.memset(xs_all[:].bitcast(I32), 0)
        nc.gpsimd.memset(w1s_raw[:].bitcast(I32), 0)

        tab_rows = tab.rearrange("(p t) j -> p t j", t=PACK)
        wa_rows = wa.rearrange("(p t) j -> p t j", t=PACK)
        tab_sb = [tile(f"tab{t}", [P, D], F32) for t in range(PACK)]
        wa_sb = tile("wa_sb", [P, PACK, D], F32)
        xw_all = tile("xw_all", [P, T], I32)
        w1w_raw = tile("w1w_raw", [P, D], I32)
        gt_sb = tile("gt_sb", [P, PACK], F32)

        nc.sync.dma_start(out=n1_sb[:], in_=n1)
        nc.sync.dma_start(out=tab_sb[0][:], in_=tab_rows[:, 0, :])
        load_scale_rows(nc.sync, xs_all, x_scales)
        nc.sync.dma_start(out=tab_sb[1][:], in_=tab_rows[:, 1, :])
        nc.sync.dma_start(out=wa_sb[:], in_=wa_rows)
        nc.sync.dma_start(out=offs_sb[:], in_=offs)
        nc.sync.dma_start(out=xw_all[:], in_=words_view(x_words))
        nc.sync.dma_start(out=tab_sb[2][:], in_=tab_rows[:, 2, :])
        nc.sync.dma_start(out=gt_sb[:], in_=gt.rearrange("(p t) o -> p (t o)", t=PACK))
        nc.sync.dma_start(out=tab_sb[3][:], in_=tab_rows[:, 3, :])
        nc.sync.dma_start(out=w1w_raw[:], in_=words_view(w1_words))
        load_scale_rows(nc.sync, w1s_raw, w1_scales)
        nc.sync.dma_start(out=n2_sb[:], in_=n2)
        nc.sync.dma_start(out=n3_sb[:], in_=n3)
        nc.sync.dma_start(out=n4_sb[:], in_=n4)

        kinds = {}

        def gather_kinds(t):
            for u in range(2):
                nc.vector.tensor_copy(
                    out=kinds[t][:, u * HALF : (u + 1) * HALF],
                    in_=tab_sb[t][:].indirect(cols(n1_sb, u * HALF, HALF)),
                )

        xs_dealt = tile("xs_dealt", [P, D], U8)
        xw_dealt = tile("xw_dealt", [P, D], U32)
        wa_bf = [tile(f"wa_bf{u}", [P, HALF * PACK], BF16) for u in range(2)]
        wa_codes = tile("wa_codes", [P, D], U32)
        wa_scales = tile("wa_scales", [P, D], U8)
        w1s = tile("w1s", [P, D], U8)
        w1w = tile("w1w", [P, D], I32)

        def quantize_wa(u):
            half = slice(u * HALF, (u + 1) * HALF)
            dst, src = weave_views(wa_bf[u][:], wa_sb[:, :, half])
            nc.scalar.copy(out=dst, in_=src)
            nc.vector.quantize_mx(out=wa_codes[:, half].bitcast(FP8X4), scales=wa_scales[:, half], in_=wa_bf[u][:])

        for t in range(EARLY - 1):
            kinds[t] = tile(f"kinds{t}", [P, D], F32)
        gather_kinds(0)
        gather_kinds(1)
        xs_picked = tile("xs_picked", [P, D], U8, tag="picked")
        nc.vector.tensor_copy(out=xs_picked[:], in_=xs_all[:].indirect(offs_sb[:]))
        quantize_wa(0)
        deal(xs_dealt, xs_picked)
        xw_picked = tile("xw_picked", [P, D], U32, tag="picked")
        nc.vector.tensor_copy(out=xw_picked[:], in_=xw_all[:].bitcast(U32).indirect(offs_sb[:]))
        quantize_wa(1)
        deal(xw_dealt, xw_picked)
        kinds[EARLY - 1] = tile("kinds_last", [P, D], F32, tag="picked")
        gather_kinds(EARLY - 1)
        deal(w1w, w1w_raw)
        deal(w1s, w1s_raw)

        gy = [tile(f"gy{t}", [P, D], F32) for t in range(PACK)]
        rest = [tile(f"rest{t}", [P, D], F32) for t in range(PACK)]
        for t in range(PACK):
            rows = slice(t * P, (t + 1) * P)
            y_ps = psum.tile([P, D], F32, name=f"y_ps{t}", tag=f"y_ps{t}")
            nc.tensor.matmul_mx(
                out=y_ps[:],
                lhsT=xw_dealt[:, rows].bitcast(FP8X4),
                lhsT_scale=xs_dealt[:, rows],
                rhs=wa_codes[:].bitcast(FP8X4),
                rhs_scale=wa_scales[:],
                start=True,
                stop=True,
            )
            nc.scalar.activation(out=gy[t][:], in_=y_ps[:], func=ACT.Copy, scale=gt_sb[:, t : t + 1])

        gtab = {}
        for t in range(EARLY, PACK):
            gtab[t] = tile(f"gtab{t}", [P, D], F32)
            nc.scalar.activation(out=gtab[t][:], in_=tab_sb[t][:], func=ACT.Copy, scale=gt_sb[:, t : t + 1])

        sign = tile("sign", [P, HALF, PACK], BF16)
        nc.scalar.activation(out=sign[:], in_=gt_sb[:].unsqueeze(1).to_broadcast([P, HALF, PACK]), func=ACT.Sign)

        def make_rest(t):
            if t < EARLY:
                nc.vector.scalar_tensor_tensor(
                    out=rest[t][:], in0=kinds[t][:], scalar=gt_sb[:, t : t + 1], in1=gy[t][:], op0=ALU.mult, op1=ALU.subtract
                )
            else:
                for u in range(2):
                    half = slice(u * HALF, (u + 1) * HALF)
                    nc.vector.tensor_tensor(
                        out=rest[t][:, half],
                        in0=gtab[t][:].indirect(cols(n1_sb, u * HALF, HALF)),
                        in1=gy[t][:, half],
                        op=ALU.subtract,
                    )

        diff = [tile(f"diff{c}", [P, PACK, w], F32) for c, (s, w) in enumerate(Z_CHUNKS)]
        size = [tile(f"size{c}", [P, w * PACK], BF16) for c, (s, w) in enumerate(Z_CHUNKS)]
        z_bf = [tile(f"z_bf{c}", [P, w * PACK], BF16) for c, (s, w) in enumerate(Z_CHUNKS)]
        z_codes = [tile(f"z_codes{c}", [P, w], U32) for c, (s, w) in enumerate(Z_CHUNKS)]
        z_scales = [tile(f"z_scales{c}", [P, w], U8) for c, (s, w) in enumerate(Z_CHUNKS)]
        first, last = H_ORDER[0], H_ORDER[-1]
        h_ps = {t: psum.tile([P, D], F32, name=f"h_ps{t}") for t in H_ORDER[1:]}
        h_first = [psum.tile([P, w], F32, name=f"h_first{c}", tag=f"y_ps{c}") for c, (s, w) in enumerate(Z_CHUNKS)]
        h_sb = [tile(f"h_sb{t}", [P, D], F32) for t in range(PACK)]

        def gather_diff(c, t):
            s, w = Z_CHUNKS[c]
            nc.vector.tensor_tensor(
                out=diff[c][:, t, :], in0=gy[t][:].indirect(cols(n2_sb, s, w)), in1=rest[t][:, s : s + w], op=ALU.add
            )

        def take_size(c):
            dst, src = weave_views(size[c][:], diff[c][:])
            nc.scalar.activation(out=dst, in_=src, func=ACT.Abs)

        def apply_sign(c):
            s, w = Z_CHUNKS[c]
            nc.vector.tensor_tensor(
                out=z_bf[c][:], in0=size[c][:], in1=sign[:, :w, :].rearrange("p j t -> p (j t)"), op=ALU.mult
            )

        def second_product(c):
            s, w = Z_CHUNKS[c]
            nc.vector.quantize_mx(out=z_codes[c][:].bitcast(FP8X4), scales=z_scales[c][:], in_=z_bf[c][:])
            for t in H_ORDER:
                rows = slice(t * P, (t + 1) * P)
                nc.tensor.matmul_mx(
                    out=h_first[c][:] if t == first else h_ps[t][:, s : s + w],
                    lhsT=w1w[:, rows].bitcast(FP8X4),
                    lhsT_scale=w1s[:, rows],
                    rhs=z_codes[c][:].bitcast(FP8X4),
                    rhs_scale=z_scales[c][:],
                    start=True,
                    stop=True,
                )

        def leave_early(c):
            s, w = Z_CHUNKS[c]
            nc.scalar.copy(out=h_sb[first][:, s : s + w], in_=h_first[c][:])

        make_rest(0)
        for t in range(PACK):
            if t + 1 < PACK:
                make_rest(t + 1)
            gather_diff(0, t)
        take_size(0)
        for t in range(PACK):
            gather_diff(1, t)
        take_size(1)
        apply_sign(0)
        gather_diff(2, 0)
        second_product(0)
        for t in range(1, PACK):
            gather_diff(2, t)
        leave_early(0)
        take_size(2)
        apply_sign(1)
        second_product(1)
        leave_early(1)
        apply_sign(2)
        second_product(2)
        leave_early(2)

        pa = [tile(f"pa{t}", [P, W], F32) for t in range(PACK)]
        pb = [tile(f"pb{t}", [P, W], F32) for t in range(PACK)]
        ra = [tile(f"ra{t}", [P, W], F32) for t in range(PACK)]
        out_bf = tile("out_bf", [P, D, PACK], BF16)
        out_rows = out_0.rearrange("(p t) j -> p t j", t=PACK)
        placed = {}

        def leave_psum(t):
            nc.scalar.copy(out=h_sb[t][:], in_=h_ps[t][:])

        def fill_window(t):
            placed[t] = tile(f"placed{t}", [P, D], F32, tag=f"ra{H_ORDER[0]}" if t == H_ORDER[-1] else "")
            nc.scalar.copy(out=placed[t][:], in_=h_sb[t][:])

        def gather_a(t):
            nc.vector.tensor_copy(out=pa[t][:], in_=h_sb[t][:].indirect(n3_sb[:]))

        def gather_b(t):
            nc.vector.tensor_copy(out=pb[t][:], in_=h_sb[t][:].indirect(n4_sb[:]))

        def larger(t):
            nc.vector.tensor_tensor(out=ra[t][:], in0=pa[t][:], in1=pb[t][:], op=ALU.max)

        def place(t):
            nc.vector.tensor_copy(out=placed[t][:].indirect(n3_sb[:]), in_=ra[t][:])
            nc.sync.dma_start(out=out_rows[:, t, :], in_=placed[t][:])

        for t in H_ORDER[1:]:
            leave_psum(t)
        gather_a(first)
        gather_b(first)
        for t in H_ORDER[:-1]:
            fill_window(t)
        second, third = H_ORDER[1], H_ORDER[2]

        def regroup(t):
            nc.scalar.copy(out=out_bf[:, :, t], in_=placed[t][:])

        gather_a(second)
        larger(first)
        gather_b(second)
        place(first)
        regroup(first)
        fill_window(last)
        gather_a(third)
        larger(second)
        gather_b(third)
        gather_a(last)
        larger(third)
        gather_b(last)
        place(second)
        regroup(second)
        larger(last)
        place(third)
        regroup(third)
        place(last)

        nc.vector.tensor_copy(out=out_bf[:, :HALF, last], in_=placed[last][:, :HALF])
        nc.vector.tensor_copy(out=out_bf[:, HALF:LAST_SPLIT, last], in_=placed[last][:, HALF:LAST_SPLIT])
        nc.scalar.copy(out=out_bf[:, LAST_SPLIT:, last], in_=placed[last][:, LAST_SPLIT:])

        out_codes = tile("out_codes", [P, D], I32)
        out_scales = tile("out_scales", [P, D], U8)
        for u, queue in enumerate((nc.sync, nc.scalar)):
            half = slice(u * HALF, (u + 1) * HALF)
            nc.vector.quantize_mx(
                out=out_codes[:, half].bitcast(FP8X4),
                scales=out_scales[:, half],
                in_=out_bf[:, half, :].rearrange("p j t -> p (j t)"),
            )
            queue.dma_start(out=words_view(out_1)[:, half], in_=out_codes[:, half])
        for q in range(4):
            queue = (nc.sync, nc.scalar)[q % 2]
            queue.dma_start(
                out=out_2[0, 4 * q : 4 * q + 4, :].bitcast(I32), in_=out_scales[32 * q : 32 * q + 4, :].bitcast(I32)
            )
